import numpy as np
import ml_dtypes


def mxq(x, axis, fmt="e4m3"):
    dtype, down = {"e4m3": (ml_dtypes.float8_e4m3fn, 7), "e5m2": (ml_dtypes.float8_e5m2, 14)}[fmt]
    v = np.moveaxis(np.asarray(x, np.float32).astype(ml_dtypes.bfloat16).astype(np.float64), axis, -1)
    blocks = v.reshape(v.shape[:-1] + (-1, 32))
    amax = np.abs(blocks).max(-1, keepdims=True)
    byte = np.maximum(np.where(amax > 0, np.frexp(amax)[1] - 1 + 127, 0) - down, 1)
    scale = np.exp2(byte - 127.0)
    codes = (blocks / scale).astype(np.float32).astype(dtype).astype(np.float64)
    return np.moveaxis((codes * scale).reshape(v.shape), -1, axis)


WIDE = False


def mx_kscale(k):
    if not WIDE:
        return np.ones(k)
    levels = np.array([10, -10, 5, -5, 0])
    if k % 512:
        return np.exp2(np.random.permutation(np.resize(levels, k // 32))).repeat(32)
    a = np.empty((k // 512, 16))
    for p in range(k // 512):
        a[p, :8] = np.random.permutation(np.resize(levels, 8))
        for g in range(8):
            far = levels[np.abs(levels - a[p, g]) >= 10]
            a[p, g + 8] = far[np.random.randint(len(far))]
    return np.exp2(a.ravel()).repeat(32)


def f64(x):
    return np.asarray(x).astype(np.float64)


def striped(idx):
    return np.tile(idx.reshape(-1, 16).T, (8, 1)).astype(np.uint16)


def unstriped(offs):
    return offs[:16].T.reshape(-1).astype(np.int64)


def striped8(idx):
    return np.concatenate([x.reshape(-1, 16).T for x in idx]).astype(np.uint16)


def runs(offs, k):
    lists = np.stack([offs[16 * r : 16 * r + 16].T.reshape(-1) for r in range(8)]).astype(np.int64)
    return lists[np.arange(k) % 512 // 64]


def pack_weight(w):
    k, n = w.shape
    w = f64(np.asarray(w, np.float32).astype(ml_dtypes.bfloat16)).reshape(k // 32, 32, n)
    amax = np.abs(w).max(1)
    byte = np.clip(np.where(amax > 0, np.frexp(amax)[1] - 1 + 127 - 7, 1), 1, 254)
    scaled = (w * np.exp2(127.0 - byte)[:, None, :]).reshape(k, n).astype(np.float32)
    words = np.ascontiguousarray(scaled.reshape(k // 512, 128, 4, n).transpose(0, 1, 3, 2)).astype(ml_dtypes.float8_e4m3fn).view(np.uint8)
    return words, np.ascontiguousarray(byte.astype(np.uint8).reshape(k // 512, 16, n))


def unpack_weight(words, scales):
    g, p, n, _ = words.shape
    vals = np.ascontiguousarray(words).view(ml_dtypes.float8_e4m3fn).astype(np.float64) * np.repeat(np.exp2(scales.astype(np.float64) - 127.0), 8, axis=1)[..., None]
    return vals.transpose(0, 1, 3, 2).reshape(g * 512, n)


E2M1 = np.array([0.0, 0.5, 1.0, 1.5, 2.0, 3.0, 4.0, 6.0, -0.0, -0.5, -1.0, -1.5, -2.0, -3.0, -4.0, -6.0])


def pack_fp4(w):
    k, n = w.shape
    w = f64(np.asarray(w, np.float32).astype(ml_dtypes.bfloat16)).reshape(k // 32, 32, n)
    amax = np.abs(w).max(1)
    mant, ex = np.frexp(amax / 6.0)
    byte = np.clip(np.where(amax > 0, np.where(mant > 0.5, ex, ex - 1) + 127, 1), 1, 254)
    scaled = (w * np.exp2(127.0 - byte)[:, None, :]).reshape(k, n).astype(np.float32)
    c = np.ascontiguousarray(scaled.reshape(k // 512, 128, 4, n).transpose(0, 1, 3, 2)).astype(ml_dtypes.float4_e2m1fn).view(np.uint8) & 0xF
    words = (c[..., 0::2] | (c[..., 1::2] << 4)).reshape(k // 512, 128, 2 * n)
    return np.ascontiguousarray(words), np.ascontiguousarray(byte.astype(np.uint8).reshape(k // 512, 16, n))


def unpack_fp4(words, scales):
    g, _, n = scales.shape
    words = np.ascontiguousarray(words).reshape(g, 128, n, 2)
    nib = np.empty((g, 128, n, 4), np.uint8)
    nib[..., 0::2] = words & 0xF
    nib[..., 1::2] = words >> 4
    vals = E2M1[nib] * np.repeat(np.exp2(scales.astype(np.float64) - 127.0), 8, axis=1)[..., None]
    return vals.transpose(0, 1, 3, 2).reshape(g * 512, n)


def relu(v):
    return np.maximum(v, 0.0)

def planes(y):
    n, m = y.shape
    v = y.astype(np.float32).astype(ml_dtypes.bfloat16).astype(np.float64).reshape(n // 32, 32, m)
    top = np.abs(v).max(1)
    byte = np.clip(np.where(top > 0, np.frexp(top)[1] - 1 + 127 - 7, 1), 1, 254)
    codes = (v * np.exp2(127.0 - byte)[:, None, :]).reshape(n, m).astype(np.float32).astype(ml_dtypes.float8_e4m3fn).view(np.uint8)
    words = codes.reshape(n // 512, 128, 4, m).transpose(0, 1, 3, 2)
    return np.ascontiguousarray(words), np.ascontiguousarray(byte.astype(np.uint8).reshape(n // 512, 16, m))


K, T, S, V, N, G, H = 512, 2048, 512, 256, 512, 2048, 512


def setup_inputs():
    n = np.random.standard_normal
    s = mx_kscale(K)[:, None]
    u = mx_kscale(H)
    packed_xT = pack_weight(n((K, T)) * s)
    packed_dT = pack_weight(n((K, G)) / s)
    packed_w1 = pack_fp4(n((H, N)) / np.sqrt(H) / u[:, None])
    perm = np.stack([np.random.permutation(S) for _ in range(8)])
    return {
        "x_words": packed_xT[0],
        "x_scales": packed_xT[1],
        "d_words": packed_dT[0],
        "d_scales": packed_dT[1],
        "gn": (np.random.uniform(0.5, 1.5, (H, 1)) * u[:, None]).astype(np.float32),
        "w1_words": packed_w1[0],
        "w1_scales": packed_w1[1],
        "offs": striped(np.random.permutation(T)[:S]),
        "kidx": striped8(np.random.randint(0, G, (8, H))),
        "la": striped8(perm[:, :V]),
        "lb": striped8(perm[:, V:]),
    }


def reference(x_words, x_scales, d_words, d_scales, gn, w1_words, w1_scales, offs, kidx, la, lb):
    d_kidx = unpack_weight(d_words, d_scales)[np.arange(K)[:, None], runs(kidx, K)]
    xq = unpack_weight(x_words, x_scales)[:, unstriped(offs)]
    s = 0.0625 * (d_kidx.T @ xq)
    b = s[np.arange(H)[:, None], runs(lb, H)]
    a = s[np.arange(H)[:, None], runs(la, H)]
    wb = relu(b - a)
    wa = relu(a - b)
    d1 = np.zeros((H, S))
    d1[np.arange(H)[:, None], runs(la, H)] = wa
    d2 = d1.copy()
    d2[np.arange(H)[:, None], runs(lb, H)] = wb
    z = f64(gn) * d2
    out_0 = unpack_fp4(w1_words, w1_scales).T @ mxq(z, 0, "e4m3")
    return (out_0,) + planes(out_0)

@@ -1,0 +1,188 @@
+from contextlib import ExitStack
+
+import concourse.mybir as mybir
+
+K, T, S, V, N, G, H = 512, 2048, 512, 256, 512, 2048, 512
+FLOPS = 2 * K * H * S + 2 * H * N * S
+
+F32 = mybir.dt.float32
+BF16 = mybir.dt.bfloat16
+I32 = mybir.dt.int32
+U32 = mybir.dt.uint32
+U16 = mybir.dt.uint16
+U8 = mybir.dt.uint8
+FP8X4 = mybir.dt.float8_e4m3fn_x4
+FP4X4 = mybir.dt.float4_e2m1fn_x4
+ALU = mybir.AluOpType
+ACT = mybir.ActivationFunctionType
+
+P = 128
+PACK = 4
+HALF = S // 2
+ORDER = (2, 0, 1, 3)
+CHUNK = 128
+NCH = S // CHUNK
+
+
+def tile_picked_scorefight_none_po_kernel(
+    tc, x_words, x_scales, d_words, d_scales, gn, w1_words, w1_scales, offs, kidx, la, lb, out_0, out_1, out_2
+):
+    nc = tc.nc
+    with ExitStack() as ctx:
+        keep = ctx.enter_context(tc.tile_pool(name="keep", bufs=1))
+        ring = ctx.enter_context(tc.tile_pool(name="ring", bufs=3))
+        psum = ctx.enter_context(tc.psum_pool(name="psum", bufs=1))
+
+        kidx_sb = keep.tile([P, H // 16], U16, name="kidx_sb")
+        offs_sb = keep.tile([P, S // 16], U16, name="offs_sb")
+        la_sb = keep.tile([P, V // 16], U16, name="la_sb")
+        lb_sb = keep.tile([P, V // 16], U16, name="lb_sb")
+        dw_tab = keep.tile([P, G], U32, name="dw_tab", align_bytes=64)
+        xw_tab = keep.tile([P, T], U32, name="xw_tab", tag="x_then_w1", align_bytes=64)
+        ds_tab = keep.tile([P, G], U8, name="ds_tab", tag="d_then_w1", align_bytes=64)
+        xs_tab = keep.tile([P, T], U8, name="xs_tab", align_bytes=64)
+        w1s_raw = keep.tile([P, N], U8, name="w1s_raw", align_bytes=64)
+        gn_sb = keep.tile([P, PACK], F32, name="gn_sb")
+        ds_mm = keep.tile([P, H], U8, name="ds_mm", align_bytes=64)
+
+        nc.vector.memset(xs_tab[:].bitcast(I32), 0)
+        nc.vector.memset(ds_mm[:].bitcast(I32), 0)
+        nc.vector.memset(w1s_raw[:].bitcast(I32), 0)
+
+        nc.sync.dma_start(kidx_sb[:], kidx)
+        nc.sync.dma_start(ds_tab[:].bitcast(I32), d_scales[0].bitcast(I32).unsqueeze(1).to_broadcast([16, 8, G // 4]))
+        nc.sync.dma_start(offs_sb[:], offs)
+        nc.sync.dma_start(dw_tab[:].bitcast(I32), d_words[0].rearrange("p n t -> p (n t)").bitcast(I32))
+        for q in range(4):
+            queue = nc.gpsimd if q == 0 else nc.sync
+            queue.dma_start(xs_tab[:].bitcast(I32)[32 * q : 32 * q + 4, :], x_scales[0].bitcast(I32)[4 * q : 4 * q + 4, :])
+        nc.sync.dma_start(xw_tab[:].bitcast(I32), x_words[0].rearrange("p n t -> p (n t)").bitcast(I32))
+        nc.sync.dma_start(la_sb[:], la)
+        nc.sync.dma_start(lb_sb[:], lb)
+        for q in range(4):
+            nc.gpsimd.dma_start(w1s_raw[:].bitcast(I32)[32 * q : 32 * q + 4, :], w1_scales[0].bitcast(I32)[4 * q : 4 * q + 4, :])
+        nc.gpsimd.dma_start(gn_sb[:], gn.rearrange("(p t) o -> p (t o)", t=PACK))
+
+        ds_got = keep.tile([P, H], U8, name="ds_got", tag="d_got", align_bytes=64)
+        nc.vector.tensor_copy(ds_got[:], ds_tab[:].indirect(kidx_sb[:]))
+        w1_raw = keep.tile([P, 2 * N], U8, name="w1_raw", tag="d_then_w1", align_bytes=64)
+        nc.gpsimd.dma_start(w1_raw[:].bitcast(I32), w1_words[0].bitcast(I32))
+        ds_dealt = keep.tile([P, H], U8, name="ds_dealt", align_bytes=64)
+        nc.vector.tensor_copy(
+            ds_dealt[:].rearrange("p (t m) -> p m t", t=PACK), ds_got[:].rearrange("p (m t) -> p m t", t=PACK)
+        )
+        for q in range(4):
+            nc.scalar.dma_start(ds_mm[:].bitcast(I32)[32 * q : 32 * q + 4, :], ds_dealt[:].bitcast(I32)[32 * q : 32 * q + 32 : 8, :])
+
+        dw_got = keep.tile([P, H], U32, name="dw_got", tag="d_got", align_bytes=64)
+        nc.vector.tensor_copy(dw_got[:], dw_tab[:].indirect(kidx_sb[:]))
+        xs_got = keep.tile([P, S], U8, name="xs_got", align_bytes=64)
+        nc.vector.tensor_copy(xs_got[:], xs_tab[:].indirect(offs_sb[:]))
+        dw_mm = keep.tile([P, H], U32, name="dw_mm", align_bytes=64)
+        nc.vector.tensor_copy(
+            dw_mm[:].rearrange("p (t m) -> p m t", t=PACK), dw_got[:].rearrange("p (m t) -> p m t", t=PACK)
+        )
+        xw_got = keep.tile([P, S], U32, name="xw_got", align_bytes=64)
+        for h in range(2):
+            nc.vector.tensor_copy(xw_got[:, h * HALF : (h + 1) * HALF], xw_tab[:].indirect(offs_sb[:, 16 * h : 16 * (h + 1)]))
+
+        w1_mm = keep.tile([P, 2 * N], U8, name="w1_mm", tag="x_then_w1", align_bytes=64)
+        nc.vector.tensor_copy(
+            w1_mm[:].rearrange("p (t m b) -> p m t b", t=PACK, b=2), w1_raw[:].rearrange("p (m t b) -> p m t b", t=PACK, b=2)
+        )
+
+        t0, t1, t2, t3 = ORDER
+        scores = {t: keep.tile([P, S], F32, name=f"score{t}", align_bytes=64) for t in ORDER}
+
+        def score(t, j0, width, bank, on_vector=False):
+            cols, tok = slice(t * P, (t + 1) * P), slice(j0, j0 + width)
+            acc = psum.tile([P, width], F32, name="s_acc", tag=f"bank{bank}")
+            nc.tensor.matmul_mx(
+                out=acc[:], lhsT=dw_mm[:, cols].bitcast(FP8X4), lhsT_scale=ds_mm[:, cols],
+                rhs=xw_got[:, tok].bitcast(FP8X4), rhs_scale=xs_got[:, tok], start=True, stop=True,
+            )
+            if on_vector:
+                nc.vector.tensor_scalar(scores[t][:, tok], acc[:], 0.0625, None, ALU.mult)
+            else:
+                nc.scalar.activation(scores[t][:, tok], acc[:], ACT.Copy, scale=0.0625)
+
+        score(t0, 0, HALF, 0)
+        score(t1, 0, HALF, 1)
+        score(t0, HALF, HALF, 2)
+        score(t1, HALF, HALF, 3, on_vector=True)
+        score(t2, 0, S, 4)
+        score(t3, 0, S, 5)
+
+        z_bf = [keep.tile([P, CHUNK, PACK], BF16, name=f"z_bf{c}", align_bytes=64) for c in range(NCH)]
+        won = {}
+
+        def fight(pair):
+            a_val = keep.tile([P, 2, V], F32, name=f"a_val{pair[0]}")
+            diff = keep.tile([P, 2, V], F32, name=f"diff{pair[0]}")
+            for i, t in enumerate(pair):
+                nc.vector.tensor_copy(a_val[:, i, :], scores[t][:].indirect(la_sb[:]))
+            for i, t in enumerate(pair):
+                nc.vector.tensor_tensor(diff[:, i, :], scores[t][:].indirect(lb_sb[:]), a_val[:, i, :], ALU.subtract)
+            won_a = keep.tile([P, 2, V], F32, name=f"won_a{pair[0]}")
+            nc.scalar.activation(won_a[:], diff[:], ACT.Relu, scale=-1.0)
+            won_b = keep.tile([P, 2, V], F32, name=f"won_b{pair[0]}")
+            nc.scalar.activation(won_b[:], diff[:], ACT.Relu)
+            won[pair] = (won_a, won_b)
+
+        def put(pair):
+            won_a, won_b = won[pair]
+            placed = [ring.tile([P, S], F32, name="placed") for t in pair]
+            for i, t in enumerate(pair):
+                nc.vector.tensor_copy(placed[i][:].indirect(la_sb[:]), won_a[:, i, :])
+            for i, t in enumerate(pair):
+                nc.vector.tensor_copy(placed[i][:].indirect(lb_sb[:]), won_b[:, i, :])
+                for c in range(NCH):
+                    src = placed[i][:, c * CHUNK : (c + 1) * CHUNK]
+                    if t == t3 and c < NCH // 2:
+                        nc.vector.tensor_scalar(z_bf[c][:, :, t], src, gn_sb[:, t : t + 1], None, ALU.mult)
+                    else:
+                        nc.scalar.activation(z_bf[c][:, :, t], src, ACT.Copy, scale=gn_sb[:, t : t + 1])
+
+        fight((t0, t1))
+        w1s_mm = keep.tile([P, N], U8, name="w1s_mm", align_bytes=64, tag=f"score{t0}")
+        nc.vector.tensor_copy(
+            w1s_mm[:].rearrange("p (t m) -> p m t", t=PACK), w1s_raw[:].rearrange("p (m t) -> p m t", t=PACK)
+        )
+        fight((t2, t3))
+        put((t0, t1))
+        put((t2, t3))
+
+        out_rows = out_0.rearrange("(p t) n -> p t n", t=PACK)
+        out_words = out_1[0].rearrange("p n t -> p (n t)").bitcast(I32)
+        y_codes = keep.tile([P, S], U32, name="y_codes", align_bytes=64)
+        y_scales = keep.tile([P, S], U8, name="y_scales", align_bytes=64)
+        z_codes, z_scales = [], []
+        for c in range(NCH):
+            z_codes.append(keep.tile([P, CHUNK], U32, name=f"z_codes{c}", align_bytes=64))
+            z_scales.append(keep.tile([P, CHUNK], U8, name=f"z_scales{c}", align_bytes=64))
+            nc.vector.quantize_mx(
+                out=z_codes[c][:].bitcast(FP8X4), scales=z_scales[c][:], in_=z_bf[c][:].rearrange("p n t -> p (n t)")
+            )
+        for c in range(NCH):
+            cols = slice(c * CHUNK, (c + 1) * CHUNK)
+            y_sb = keep.tile([P, PACK, CHUNK], F32, name=f"y_sb{c}")
+            acc = psum.tile([P, PACK, CHUNK], F32, name="y_acc", tag=f"bank{c}")
+            for t in range(PACK):
+                nc.tensor.matmul_mx(
+                    out=acc[:, t, :], lhsT=w1_mm[:, 2 * t * P : 2 * (t + 1) * P].bitcast(FP4X4),
+                    lhsT_scale=w1s_mm[:, t * P : (t + 1) * P],
+                    rhs=z_codes[c][:].bitcast(FP8X4), rhs_scale=z_scales[c][:], start=True, stop=True,
+                )
+            nc.scalar.copy(y_sb[:], acc[:])
+            nc.sync.dma_start(out_rows[:, :, cols], y_sb[:])
+            y_bf = keep.tile([P, CHUNK, PACK], BF16, name=f"y_bf{c}", align_bytes=64)
+            nc.vector.tensor_copy(y_bf[:], y_sb[:].rearrange("p t n -> p n t"))
+            nc.vector.quantize_mx(
+                out=y_codes[:, cols].bitcast(FP8X4), scales=y_scales[:, cols], in_=y_bf[:].rearrange("p n t -> p (n t)")
+            )
+            if c >= NCH - 2:
+                done = slice(0 if c == NCH - 2 else c * CHUNK, (c + 1) * CHUNK)
+                nc.sync.dma_start(out_words[:, done], y_codes[:, done].bitcast(I32))
+        for q in range(4):
+            queue = nc.scalar if q % 2 == 0 else nc.sync
+            queue.dma_start(out_2[0].bitcast(I32)[4 * q : 4 * q + 4, :], y_scales[:].bitcast(I32)[32 * q : 32 * q + 4, :])

@@ -39,8 +39,9 @@ def tile_picked_scorefight_none_po_kernel(
         lb_sb = keep.tile([P, V // 16], U16, name="lb_sb")
         dw_tab = keep.tile([P, G], U32, name="dw_tab", align_bytes=64)
         xw_tab = keep.tile([P, T], U32, name="xw_tab", tag="x_then_w1", align_bytes=64)
-        ds_tab = keep.tile([P, G], U8, name="ds_tab", tag="d_then_w1", align_bytes=64)
+        ds_tab = keep.tile([P, G], U8, name="ds_tab", align_bytes=64)
         xs_tab = keep.tile([P, T], U8, name="xs_tab", align_bytes=64)
+        w1_raw = keep.tile([P, 2 * N], U8, name="w1_raw", align_bytes=64)
         w1s_raw = keep.tile([P, N], U8, name="w1s_raw", align_bytes=64)
         gn_sb = keep.tile([P, PACK], F32, name="gn_sb")
         ds_mm = keep.tile([P, H], U8, name="ds_mm", align_bytes=64)
@@ -52,11 +53,11 @@ def tile_picked_scorefight_none_po_kernel(
         nc.sync.dma_start(kidx_sb[:], kidx)
         nc.sync.dma_start(ds_tab[:].bitcast(I32), d_scales[0].bitcast(I32).unsqueeze(1).to_broadcast([16, 8, G // 4]))
         nc.sync.dma_start(offs_sb[:], offs)
-        nc.sync.dma_start(dw_tab[:].bitcast(I32), d_words[0].rearrange("p n t -> p (n t)").bitcast(I32))
         for q in range(4):
-            queue = nc.gpsimd if q == 0 else nc.sync
-            queue.dma_start(xs_tab[:].bitcast(I32)[32 * q : 32 * q + 4, :], x_scales[0].bitcast(I32)[4 * q : 4 * q + 4, :])
+            nc.sync.dma_start(xs_tab[:].bitcast(I32)[32 * q : 32 * q + 4, :], x_scales[0].bitcast(I32)[4 * q : 4 * q + 4, :])
+        nc.sync.dma_start(dw_tab[:].bitcast(I32), d_words[0].rearrange("p n t -> p (n t)").bitcast(I32))
         nc.sync.dma_start(xw_tab[:].bitcast(I32), x_words[0].rearrange("p n t -> p (n t)").bitcast(I32))
+        nc.sync.dma_start(w1_raw[:].bitcast(I32), w1_words[0].bitcast(I32))
         nc.sync.dma_start(la_sb[:], la)
         nc.sync.dma_start(lb_sb[:], lb)
         for q in range(4):
@@ -65,8 +66,6 @@ def tile_picked_scorefight_none_po_kernel(
 
         ds_got = keep.tile([P, H], U8, name="ds_got", tag="d_got", align_bytes=64)
         nc.vector.tensor_copy(ds_got[:], ds_tab[:].indirect(kidx_sb[:]))
-        w1_raw = keep.tile([P, 2 * N], U8, name="w1_raw", tag="d_then_w1", align_bytes=64)
-        nc.gpsimd.dma_start(w1_raw[:].bitcast(I32), w1_words[0].bitcast(I32))
         ds_dealt = keep.tile([P, H], U8, name="ds_dealt", align_bytes=64)
         nc.vector.tensor_copy(
             ds_dealt[:].rearrange("p (t m) -> p m t", t=PACK), ds_got[:].rearrange("p (m t) -> p m t", t=PACK)
@@ -74,55 +73,59 @@ def tile_picked_scorefight_none_po_kernel(
         for q in range(4):
             nc.scalar.dma_start(ds_mm[:].bitcast(I32)[32 * q : 32 * q + 4, :], ds_dealt[:].bitcast(I32)[32 * q : 32 * q + 32 : 8, :])
 
-        dw_got = keep.tile([P, H], U32, name="dw_got", tag="d_got", align_bytes=64)
-        nc.vector.tensor_copy(dw_got[:], dw_tab[:].indirect(kidx_sb[:]))
         xs_got = keep.tile([P, S], U8, name="xs_got", align_bytes=64)
         nc.vector.tensor_copy(xs_got[:], xs_tab[:].indirect(offs_sb[:]))
+        dw_got = keep.tile([P, H], U32, name="dw_got", tag="d_got", align_bytes=64)
+        nc.vector.tensor_copy(dw_got[:], dw_tab[:].indirect(kidx_sb[:]))
         dw_mm = keep.tile([P, H], U32, name="dw_mm", align_bytes=64)
         nc.vector.tensor_copy(
             dw_mm[:].rearrange("p (t m) -> p m t", t=PACK), dw_got[:].rearrange("p (m t) -> p m t", t=PACK)
         )
-        xw_got = keep.tile([P, S], U32, name="xw_got", align_bytes=64)
+        xw_got = [keep.tile([P, HALF], U32, name=f"xw_got{h}", align_bytes=64) for h in range(2)]
         for h in range(2):
-            nc.vector.tensor_copy(xw_got[:, h * HALF : (h + 1) * HALF], xw_tab[:].indirect(offs_sb[:, 16 * h : 16 * (h + 1)]))
+            nc.vector.tensor_copy(xw_got[h][:], xw_tab[:].indirect(offs_sb[:, 16 * h : 16 * (h + 1)]))
 
-        w1_mm = keep.tile([P, 2 * N], U8, name="w1_mm", tag="x_then_w1", align_bytes=64)
+        w1s_mm = keep.tile([P, N], U8, name="w1s_mm", tag="x_then_w1", align_bytes=64)
         nc.vector.tensor_copy(
-            w1_mm[:].rearrange("p (t m b) -> p m t b", t=PACK, b=2), w1_raw[:].rearrange("p (m t b) -> p m t b", t=PACK, b=2)
+            w1s_mm[:].rearrange("p (t m) -> p m t", t=PACK), w1s_raw[:].rearrange("p (m t) -> p m t", t=PACK)
         )
 
         t0, t1, t2, t3 = ORDER
         scores = {t: keep.tile([P, S], F32, name=f"score{t}", align_bytes=64) for t in ORDER}
 
-        def score(t, j0, width, bank, on_vector=False):
-            cols, tok = slice(t * P, (t + 1) * P), slice(j0, j0 + width)
-            acc = psum.tile([P, width], F32, name="s_acc", tag=f"bank{bank}")
-            nc.tensor.matmul_mx(
-                out=acc[:], lhsT=dw_mm[:, cols].bitcast(FP8X4), lhsT_scale=ds_mm[:, cols],
-                rhs=xw_got[:, tok].bitcast(FP8X4), rhs_scale=xs_got[:, tok], start=True, stop=True,
-            )
+        def score(t, halves, bank, on_vector=False):
+            cols = slice(t * P, (t + 1) * P)
+            acc = psum.tile([P, len(halves), HALF], F32, name="s_acc", tag=f"bank{bank}")
+            for i, h in enumerate(halves):
+                nc.tensor.matmul_mx(
+                    out=acc[:, i, :], lhsT=dw_mm[:, cols].bitcast(FP8X4), lhsT_scale=ds_mm[:, cols],
+                    rhs=xw_got[h][:].bitcast(FP8X4), rhs_scale=xs_got[:, h * HALF : (h + 1) * HALF], start=True, stop=True,
+                )
+            dst = scores[t][:, halves[0] * HALF : (halves[-1] + 1) * HALF]
+            src = acc[:].rearrange("p h n -> p (h n)")
             if on_vector:
-                nc.vector.tensor_scalar(scores[t][:, tok], acc[:], 0.0625, None, ALU.mult)
+                nc.vector.tensor_scalar(dst, src, 0.0625, None, ALU.mult)
             else:
-                nc.scalar.activation(scores[t][:, tok], acc[:], ACT.Copy, scale=0.0625)
+                nc.scalar.activation(dst, src, ACT.Copy, scale=0.0625)
 
-        score(t0, 0, HALF, 0)
-        score(t1, 0, HALF, 1)
-        score(t0, HALF, HALF, 2)
-        score(t1, HALF, HALF, 3, on_vector=True)
-        score(t2, 0, S, 4)
-        score(t3, 0, S, 5)
+        score(t0, (0,), 0)
+        score(t1, (0,), 1)
+        score(t0, (1,), 2)
+        score(t1, (1,), 3, on_vector=False)
+        score(t2, (0, 1), 4)
+        score(t3, (0, 1), 5)
 
         z_bf = [keep.tile([P, CHUNK, PACK], BF16, name=f"z_bf{c}", align_bytes=64) for c in range(NCH)]
         won = {}
 
         def fight(pair):
             a_val = keep.tile([P, 2, V], F32, name=f"a_val{pair[0]}")
-            diff = keep.tile([P, 2, V], F32, name=f"diff{pair[0]}")
+            b_val = keep.tile([P, 2, V], F32, name=f"b_val{pair[0]}")
+            diff = keep.tile([P, 2, V], F32, name=f"diff{pair[0]}", align_bytes=64)
             for i, t in enumerate(pair):
                 nc.vector.tensor_copy(a_val[:, i, :], scores[t][:].indirect(la_sb[:]))
-            for i, t in enumerate(pair):
-                nc.vector.tensor_tensor(diff[:, i, :], scores[t][:].indirect(lb_sb[:]), a_val[:, i, :], ALU.subtract)
+                nc.vector.tensor_copy(b_val[:, i, :], scores[t][:].indirect(lb_sb[:]))
+            nc.gpsimd.tensor_tensor(diff[:], b_val[:], a_val[:], ALU.subtract)
             won_a = keep.tile([P, 2, V], F32, name=f"won_a{pair[0]}")
             nc.scalar.activation(won_a[:], diff[:], ACT.Relu, scale=-1.0)
             won_b = keep.tile([P, 2, V], F32, name=f"won_b{pair[0]}")
@@ -144,11 +147,11 @@ def tile_picked_scorefight_none_po_kernel(
                         nc.scalar.activation(z_bf[c][:, :, t], src, ACT.Copy, scale=gn_sb[:, t : t + 1])
 
         fight((t0, t1))
-        w1s_mm = keep.tile([P, N], U8, name="w1s_mm", align_bytes=64, tag=f"score{t0}")
-        nc.vector.tensor_copy(
-            w1s_mm[:].rearrange("p (t m) -> p m t", t=PACK), w1s_raw[:].rearrange("p (m t) -> p m t", t=PACK)
-        )
         fight((t2, t3))
+        w1_mm = keep.tile([P, 2 * N], U8, name="w1_mm", tag=f"diff{t2}", align_bytes=64)
+        nc.gpsimd.tensor_copy(
+            w1_mm[:].rearrange("p (t m b) -> p m t b", t=PACK, b=2), w1_raw[:].rearrange("p (m t b) -> p m t b", t=PACK, b=2)
+        )
         put((t0, t1))
         put((t2, t3))
 
@@ -166,14 +169,16 @@ def tile_picked_scorefight_none_po_kernel(
         for c in range(NCH):
             cols = slice(c * CHUNK, (c + 1) * CHUNK)
             y_sb = keep.tile([P, PACK, CHUNK], F32, name=f"y_sb{c}")
-            acc = psum.tile([P, PACK, CHUNK], F32, name="y_acc", tag=f"bank{c}")
-            for t in range(PACK):
-                nc.tensor.matmul_mx(
-                    out=acc[:, t, :], lhsT=w1_mm[:, 2 * t * P : 2 * (t + 1) * P].bitcast(FP4X4),
-                    lhsT_scale=w1s_mm[:, t * P : (t + 1) * P],
-                    rhs=z_codes[c][:].bitcast(FP8X4), rhs_scale=z_scales[c][:], start=True, stop=True,
-                )
-            nc.scalar.copy(y_sb[:], acc[:])
+            for u in range(2):
+                acc = psum.tile([P, 2, CHUNK], F32, name="y_acc", tag=f"bank{2 * c + u}")
+                for e in range(2):
+                    t = 2 * u + e
+                    nc.tensor.matmul_mx(
+                        out=acc[:, e, :], lhsT=w1_mm[:, 2 * t * P : 2 * (t + 1) * P].bitcast(FP4X4),
+                        lhsT_scale=w1s_mm[:, t * P : (t + 1) * P],
+                        rhs=z_codes[c][:].bitcast(FP8X4), rhs_scale=z_scales[c][:], start=True, stop=True,
+                    )
+                nc.scalar.copy(y_sb[:, 2 * u : 2 * u + 2, :], acc[:])
             nc.sync.dma_start(out_rows[:, :, cols], y_sb[:])
             y_bf = keep.tile([P, CHUNK, PACK], BF16, name=f"y_bf{c}", align_bytes=64)
             nc.vector.tensor_copy(y_bf[:], y_sb[:].rearrange("p t n -> p n t"))

@@ -46,13 +46,14 @@ def tile_picked_scorefight_none_po_kernel(
         gn_sb = keep.tile([P, PACK], F32, name="gn_sb")
         ds_mm = keep.tile([P, H], U8, name="ds_mm", align_bytes=64)
 
+        nc.vector.memset(ds_tab[:].bitcast(I32), 0)
         nc.vector.memset(xs_tab[:].bitcast(I32), 0)
         nc.vector.memset(ds_mm[:].bitcast(I32), 0)
         nc.vector.memset(w1s_raw[:].bitcast(I32), 0)
 
         nc.sync.dma_start(kidx_sb[:], kidx)
-        nc.sync.dma_start(ds_tab[:].bitcast(I32), d_scales[0].bitcast(I32).unsqueeze(1).to_broadcast([16, 8, G // 4]))
         nc.sync.dma_start(offs_sb[:], offs)
+        nc.sync.dma_start(ds_tab[:].bitcast(I32)[0:P:8, :], d_scales[0].bitcast(I32))
         for q in range(4):
             nc.sync.dma_start(xs_tab[:].bitcast(I32)[32 * q : 32 * q + 4, :], x_scales[0].bitcast(I32)[4 * q : 4 * q + 4, :])
         nc.sync.dma_start(dw_tab[:].bitcast(I32), d_words[0].rearrange("p n t -> p (n t)").bitcast(I32))
@@ -139,12 +140,11 @@ def tile_picked_scorefight_none_po_kernel(
                 nc.vector.tensor_copy(placed[i][:].indirect(la_sb[:]), won_a[:, i, :])
             for i, t in enumerate(pair):
                 nc.vector.tensor_copy(placed[i][:].indirect(lb_sb[:]), won_b[:, i, :])
-                for c in range(NCH):
-                    src = placed[i][:, c * CHUNK : (c + 1) * CHUNK]
-                    if t == t3 and c < NCH // 2:
-                        nc.vector.tensor_scalar(z_bf[c][:, :, t], src, gn_sb[:, t : t + 1], None, ALU.mult)
-                    else:
+                if t != t3:
+                    for c in range(NCH):
+                        src = placed[i][:, c * CHUNK : (c + 1) * CHUNK]
                         nc.scalar.activation(z_bf[c][:, :, t], src, ACT.Copy, scale=gn_sb[:, t : t + 1])
+            return placed[-1]
 
         fight((t0, t1))
         fight((t2, t3))
@@ -153,19 +153,26 @@ def tile_picked_scorefight_none_po_kernel(
             w1_mm[:].rearrange("p (t m b) -> p m t b", t=PACK, b=2), w1_raw[:].rearrange("p (m t b) -> p m t b", t=PACK, b=2)
         )
         put((t0, t1))
-        put((t2, t3))
+        last = put((t2, t3))
 
         out_rows = out_0.rearrange("(p t) n -> p t n", t=PACK)
         out_words = out_1[0].rearrange("p n t -> p (n t)").bitcast(I32)
         y_codes = keep.tile([P, S], U32, name="y_codes", align_bytes=64)
         y_scales = keep.tile([P, S], U8, name="y_scales", align_bytes=64)
-        z_codes, z_scales = [], []
-        for c in range(NCH):
-            z_codes.append(keep.tile([P, CHUNK], U32, name=f"z_codes{c}", align_bytes=64))
-            z_scales.append(keep.tile([P, CHUNK], U8, name=f"z_scales{c}", align_bytes=64))
-            nc.vector.quantize_mx(
-                out=z_codes[c][:].bitcast(FP8X4), scales=z_scales[c][:], in_=z_bf[c][:].rearrange("p n t -> p (n t)")
-            )
+        z_codes = [keep.tile([P, CHUNK], U32, name=f"z_codes{c}", align_bytes=64) for c in range(NCH)]
+        z_scales = [keep.tile([P, CHUNK], U8, name=f"z_scales{c}", align_bytes=64) for c in range(NCH)]
+        for c in range(NCH + 1):
+            if c < NCH:
+                src = last[:, c * CHUNK : (c + 1) * CHUNK]
+                if c < NCH // 2:
+                    nc.vector.tensor_scalar(z_bf[c][:, :, t3], src, gn_sb[:, t3 : t3 + 1], None, ALU.mult)
+                else:
+                    nc.scalar.activation(z_bf[c][:, :, t3], src, ACT.Copy, scale=gn_sb[:, t3 : t3 + 1])
+            if c > 0:
+                nc.vector.quantize_mx(
+                    out=z_codes[c - 1][:].bitcast(FP8X4), scales=z_scales[c - 1][:],
+                    in_=z_bf[c - 1][:].rearrange("p n t -> p (n t)"),
+                )
         for c in range(NCH):
             cols = slice(c * CHUNK, (c + 1) * CHUNK)
             y_sb = keep.tile([P, PACK, CHUNK], F32, name=f"y_sb{c}")
@@ -179,7 +186,10 @@ def tile_picked_scorefight_none_po_kernel(
                         rhs=z_codes[c][:].bitcast(FP8X4), rhs_scale=z_scales[c][:], start=True, stop=True,
                     )
                 nc.scalar.copy(y_sb[:, 2 * u : 2 * u + 2, :], acc[:])
-            nc.sync.dma_start(out_rows[:, :, cols], y_sb[:])
+                if c == 0:
+                    nc.sync.dma_start(out_rows[:, 2 * u : 2 * u + 2, cols], y_sb[:, 2 * u : 2 * u + 2, :])
+            if c > 0:
+                nc.sync.dma_start(out_rows[:, :, cols], y_sb[:])
             y_bf = keep.tile([P, CHUNK, PACK], BF16, name=f"y_bf{c}", align_bytes=64)
             nc.vector.tensor_copy(y_bf[:], y_sb[:].rearrange("p t n -> p n t"))
             nc.vector.quantize_mx(

from contextlib import ExitStack

import concourse.mybir as mybir

K, T, S, V, N, G, H = 512, 2048, 512, 256, 512, 2048, 512
FLOPS = 2 * K * H * S + 2 * H * N * S

F32 = mybir.dt.float32
BF16 = mybir.dt.bfloat16
I32 = mybir.dt.int32
U32 = mybir.dt.uint32
U16 = mybir.dt.uint16
U8 = mybir.dt.uint8
FP8X4 = mybir.dt.float8_e4m3fn_x4
FP4X4 = mybir.dt.float4_e2m1fn_x4
ALU = mybir.AluOpType
ACT = mybir.ActivationFunctionType

P = 128
PACK = 4
HALF = S // 2
ORDER = (2, 0, 1, 3)
CHUNK = 128
NCH = S // CHUNK


def tile_picked_scorefight_none_po_kernel(
    tc, x_words, x_scales, d_words, d_scales, gn, w1_words, w1_scales, offs, kidx, la, lb, out_0, out_1, out_2
):
    nc = tc.nc
    with ExitStack() as ctx:
        keep = ctx.enter_context(tc.tile_pool(name="keep", bufs=1))
        ring = ctx.enter_context(tc.tile_pool(name="ring", bufs=3))
        psum = ctx.enter_context(tc.psum_pool(name="psum", bufs=1))

        kidx_sb = keep.tile([P, H // 16], U16, name="kidx_sb")
        offs_sb = keep.tile([P, S // 16], U16, name="offs_sb")
        la_sb = keep.tile([P, V // 16], U16, name="la_sb")
        lb_sb = keep.tile([P, V // 16], U16, name="lb_sb")
        dw_tab = keep.tile([P, G], U32, name="dw_tab", align_bytes=64)
        xw_tab = keep.tile([P, T], U32, name="xw_tab", tag="x_then_w1", align_bytes=64)
        ds_tab = keep.tile([P, G], U8, name="ds_tab", align_bytes=64)
        xs_tab = keep.tile([P, T], U8, name="xs_tab", align_bytes=64)
        w1_raw = keep.tile([P, 2 * N], U8, name="w1_raw", align_bytes=64)
        w1s_raw = keep.tile([P, N], U8, name="w1s_raw", align_bytes=64)
        gn_sb = keep.tile([P, PACK], F32, name="gn_sb")
        ds_mm = keep.tile([P, H], U8, name="ds_mm", align_bytes=64)

        nc.vector.memset(ds_tab[:].bitcast(I32), 0)
        nc.vector.memset(xs_tab[:].bitcast(I32), 0)
        nc.vector.memset(ds_mm[:].bitcast(I32), 0)
        nc.vector.memset(w1s_raw[:].bitcast(I32), 0)

        nc.sync.dma_start(kidx_sb[:], kidx)
        nc.sync.dma_start(offs_sb[:], offs)
        nc.sync.dma_start(ds_tab[:].bitcast(I32)[0:P:8, :], d_scales[0].bitcast(I32))
        for q in range(4):
            nc.sync.dma_start(xs_tab[:].bitcast(I32)[32 * q : 32 * q + 4, :], x_scales[0].bitcast(I32)[4 * q : 4 * q + 4, :])
        nc.sync.dma_start(dw_tab[:].bitcast(I32), d_words[0].rearrange("p n t -> p (n t)").bitcast(I32))
        nc.sync.dma_start(xw_tab[:].bitcast(I32), x_words[0].rearrange("p n t -> p (n t)").bitcast(I32))
        nc.sync.dma_start(w1_raw[:].bitcast(I32), w1_words[0].bitcast(I32))
        nc.sync.dma_start(la_sb[:], la)
        nc.sync.dma_start(lb_sb[:], lb)
        for q in range(4):
            nc.gpsimd.dma_start(w1s_raw[:].bitcast(I32)[32 * q : 32 * q + 4, :], w1_scales[0].bitcast(I32)[4 * q : 4 * q + 4, :])
        nc.gpsimd.dma_start(gn_sb[:], gn.rearrange("(p t) o -> p (t o)", t=PACK))

        ds_got = keep.tile([P, H], U8, name="ds_got", tag="d_got", align_bytes=64)
        nc.vector.tensor_copy(ds_got[:], ds_tab[:].indirect(kidx_sb[:]))
        ds_dealt = keep.tile([P, H], U8, name="ds_dealt", align_bytes=64)
        nc.vector.tensor_copy(
            ds_dealt[:].rearrange("p (t m) -> p m t", t=PACK), ds_got[:].rearrange("p (m t) -> p m t", t=PACK)
        )
        for q in range(4):
            nc.scalar.dma_start(ds_mm[:].bitcast(I32)[32 * q : 32 * q + 4, :], ds_dealt[:].bitcast(I32)[32 * q : 32 * q + 32 : 8, :])

        xs_got = keep.tile([P, S], U8, name="xs_got", align_bytes=64)
        nc.vector.tensor_copy(xs_got[:], xs_tab[:].indirect(offs_sb[:]))
        dw_got = keep.tile([P, H], U32, name="dw_got", tag="d_got", align_bytes=64)
        nc.vector.tensor_copy(dw_got[:], dw_tab[:].indirect(kidx_sb[:]))
        dw_mm = keep.tile([P, H], U32, name="dw_mm", align_bytes=64)
        nc.vector.tensor_copy(
            dw_mm[:].rearrange("p (t m) -> p m t", t=PACK), dw_got[:].rearrange("p (m t) -> p m t", t=PACK)
        )
        xw_got = [keep.tile([P, HALF], U32, name=f"xw_got{h}", align_bytes=64) for h in range(2)]
        for h in range(2):
            nc.vector.tensor_copy(xw_got[h][:], xw_tab[:].indirect(offs_sb[:, 16 * h : 16 * (h + 1)]))

        w1s_mm = keep.tile([P, N], U8, name="w1s_mm", tag="x_then_w1", align_bytes=64)
        nc.vector.tensor_copy(
            w1s_mm[:].rearrange("p (t m) -> p m t", t=PACK), w1s_raw[:].rearrange("p (m t) -> p m t", t=PACK)
        )

        t0, t1, t2, t3 = ORDER
        scores = {t: keep.tile([P, S], F32, name=f"score{t}", align_bytes=64) for t in ORDER}

        def score(t, halves, bank, on_vector=False):
            cols = slice(t * P, (t + 1) * P)
            acc = psum.tile([P, len(halves), HALF], F32, name="s_acc", tag=f"bank{bank}")
            for i, h in enumerate(halves):
                nc.tensor.matmul_mx(
                    out=acc[:, i, :], lhsT=dw_mm[:, cols].bitcast(FP8X4), lhsT_scale=ds_mm[:, cols],
                    rhs=xw_got[h][:].bitcast(FP8X4), rhs_scale=xs_got[:, h * HALF : (h + 1) * HALF], start=True, stop=True,
                )
            dst = scores[t][:, halves[0] * HALF : (halves[-1] + 1) * HALF]
            src = acc[:].rearrange("p h n -> p (h n)")
            if on_vector:
                nc.vector.tensor_scalar(dst, src, 0.0625, None, ALU.mult)
            else:
                nc.scalar.activation(dst, src, ACT.Copy, scale=0.0625)

        score(t0, (0,), 0)
        score(t1, (0,), 1)
        score(t0, (1,), 2)
        score(t1, (1,), 3, on_vector=False)
        score(t2, (0, 1), 4)
        score(t3, (0, 1), 5)

        z_bf = [keep.tile([P, CHUNK, PACK], BF16, name=f"z_bf{c}", align_bytes=64) for c in range(NCH)]
        won = {}

        def fight(pair):
            a_val = keep.tile([P, 2, V], F32, name=f"a_val{pair[0]}")
            b_val = keep.tile([P, 2, V], F32, name=f"b_val{pair[0]}")
            diff = keep.tile([P, 2, V], F32, name=f"diff{pair[0]}", align_bytes=64)
            for i, t in enumerate(pair):
                nc.vector.tensor_copy(a_val[:, i, :], scores[t][:].indirect(la_sb[:]))
                nc.vector.tensor_copy(b_val[:, i, :], scores[t][:].indirect(lb_sb[:]))
            nc.gpsimd.tensor_tensor(diff[:], b_val[:], a_val[:], ALU.subtract)
            won_a = keep.tile([P, 2, V], F32, name=f"won_a{pair[0]}")
            nc.scalar.activation(won_a[:], diff[:], ACT.Relu, scale=-1.0)
            won_b = keep.tile([P, 2, V], F32, name=f"won_b{pair[0]}")
            nc.scalar.activation(won_b[:], diff[:], ACT.Relu)
            won[pair] = (won_a, won_b)

        def put(pair):
            won_a, won_b = won[pair]
            placed = [ring.tile([P, S], F32, name="placed") for t in pair]
            for i, t in enumerate(pair):
                nc.vector.tensor_copy(placed[i][:].indirect(la_sb[:]), won_a[:, i, :])
            for i, t in enumerate(pair):
                nc.vector.tensor_copy(placed[i][:].indirect(lb_sb[:]), won_b[:, i, :])
                if t != t3:
                    for c in range(NCH):
                        src = placed[i][:, c * CHUNK : (c + 1) * CHUNK]
                        nc.scalar.activation(z_bf[c][:, :, t], src, ACT.Copy, scale=gn_sb[:, t : t + 1])
            return placed[-1]

        fight((t0, t1))
        fight((t2, t3))
        w1_mm = keep.tile([P, 2 * N], U8, name="w1_mm", tag=f"diff{t2}", align_bytes=64)
        nc.gpsimd.tensor_copy(
            w1_mm[:].rearrange("p (t m b) -> p m t b", t=PACK, b=2), w1_raw[:].rearrange("p (m t b) -> p m t b", t=PACK, b=2)
        )
        put((t0, t1))
        last = put((t2, t3))

        out_rows = out_0.rearrange("(p t) n -> p t n", t=PACK)
        out_words = out_1[0].rearrange("p n t -> p (n t)").bitcast(I32)
        y_codes = keep.tile([P, S], U32, name="y_codes", align_bytes=64)
        y_scales = keep.tile([P, S], U8, name="y_scales", align_bytes=64)
        z_codes = [keep.tile([P, CHUNK], U32, name=f"z_codes{c}", align_bytes=64) for c in range(NCH)]
        z_scales = [keep.tile([P, CHUNK], U8, name=f"z_scales{c}", align_bytes=64) for c in range(NCH)]
        for c in range(NCH + 1):
            if c < NCH:
                src = last[:, c * CHUNK : (c + 1) * CHUNK]
                if c < NCH // 2:
                    nc.vector.tensor_scalar(z_bf[c][:, :, t3], src, gn_sb[:, t3 : t3 + 1], None, ALU.mult)
                else:
                    nc.scalar.activation(z_bf[c][:, :, t3], src, ACT.Copy, scale=gn_sb[:, t3 : t3 + 1])
            if c > 0:
                nc.vector.quantize_mx(
                    out=z_codes[c - 1][:].bitcast(FP8X4), scales=z_scales[c - 1][:],
                    in_=z_bf[c - 1][:].rearrange("p n t -> p (n t)"),
                )
        for c in range(NCH):
            cols = slice(c * CHUNK, (c + 1) * CHUNK)
            y_sb = keep.tile([P, PACK, CHUNK], F32, name=f"y_sb{c}")
            for u in range(2):
                acc = psum.tile([P, 2, CHUNK], F32, name="y_acc", tag=f"bank{2 * c + u}")
                for e in range(2):
                    t = 2 * u + e
                    nc.tensor.matmul_mx(
                        out=acc[:, e, :], lhsT=w1_mm[:, 2 * t * P : 2 * (t + 1) * P].bitcast(FP4X4),
                        lhsT_scale=w1s_mm[:, t * P : (t + 1) * P],
                        rhs=z_codes[c][:].bitcast(FP8X4), rhs_scale=z_scales[c][:], start=True, stop=True,
                    )
                nc.scalar.copy(y_sb[:, 2 * u : 2 * u + 2, :], acc[:])
                if c == 0:
                    nc.sync.dma_start(out_rows[:, 2 * u : 2 * u + 2, cols], y_sb[:, 2 * u : 2 * u + 2, :])
            if c > 0:
                nc.sync.dma_start(out_rows[:, :, cols], y_sb[:])
            y_bf = keep.tile([P, CHUNK, PACK], BF16, name=f"y_bf{c}", align_bytes=64)
            nc.vector.tensor_copy(y_bf[:], y_sb[:].rearrange("p t n -> p n t"))
            nc.vector.quantize_mx(
                out=y_codes[:, cols].bitcast(FP8X4), scales=y_scales[:, cols], in_=y_bf[:].rearrange("p n t -> p (n t)")
            )
            if c >= NCH - 2:
                done = slice(0 if c == NCH - 2 else c * CHUNK, (c + 1) * CHUNK)
                nc.sync.dma_start(out_words[:, done], y_codes[:, done].bitcast(I32))
        for q in range(4):
            queue = nc.scalar if q % 2 == 0 else nc.sync
            queue.dma_start(out_2[0].bitcast(I32)[4 * q : 4 * q + 4, :], y_scales[:].bitcast(I32)[32 * q : 32 * q + 4, :])
